import numpy as np
import ml_dtypes


def mxq(x, axis, fmt="e4m3"):
    dtype, down = {"e4m3": (ml_dtypes.float8_e4m3fn, 7), "e5m2": (ml_dtypes.float8_e5m2, 14)}[fmt]
    v = np.moveaxis(np.asarray(x, np.float32).astype(ml_dtypes.bfloat16).astype(np.float64), axis, -1)
    blocks = v.reshape(v.shape[:-1] + (-1, 32))
    amax = np.abs(blocks).max(-1, keepdims=True)
    byte = np.maximum(np.where(amax > 0, np.frexp(amax)[1] - 1 + 127, 0) - down, 1)
    scale = np.exp2(byte - 127.0)
    codes = (blocks / scale).astype(np.float32).astype(dtype).astype(np.float64)
    return np.moveaxis((codes * scale).reshape(v.shape), -1, axis)


WIDE = False


def mx_kscale(k):
    if not WIDE:
        return np.ones(k)
    levels = np.array([10, -10, 5, -5, 0])
    if k % 512:
        return np.exp2(np.random.permutation(np.resize(levels, k // 32))).repeat(32)
    a = np.empty((k // 512, 16))
    for p in range(k // 512):
        a[p, :8] = np.random.permutation(np.resize(levels, 8))
        for g in range(8):
            far = levels[np.abs(levels - a[p, g]) >= 10]
            a[p, g + 8] = far[np.random.randint(len(far))]
    return np.exp2(a.ravel()).repeat(32)


BF16 = ml_dtypes.bfloat16


def bf(x):
    return np.asarray(x, np.float32).astype(BF16)


def f64(x):
    return np.asarray(x).astype(np.float64)


E2M1 = np.array([0.0, 0.5, 1.0, 1.5, 2.0, 3.0, 4.0, 6.0, -0.0, -0.5, -1.0, -1.5, -2.0, -3.0, -4.0, -6.0])


def pack_weight(w, fmt):
    k, n = w.shape
    w = f64(bf(w)).reshape(k // 32, 32, n)
    amax = np.abs(w).max(1)
    if fmt == "e4m3":
        byte = np.frexp(amax)[1] - 1 + 127 - 7
    else:
        mant, ex = np.frexp(amax / 6.0)
        byte = np.where(mant > 0.5, ex, ex - 1) + 127
    byte = np.clip(np.where(amax > 0, byte, 1), 1, 254)
    scaled = (w * np.exp2(127.0 - byte)[:, None, :]).reshape(k, n).astype(np.float32)
    by_word = np.ascontiguousarray(scaled.reshape(k // 512, 128, 4, n).transpose(0, 1, 3, 2))
    if fmt == "e4m3":
        words = by_word.astype(ml_dtypes.float8_e4m3fn).view(np.uint8)
    else:
        c = by_word.astype(ml_dtypes.float4_e2m1fn).view(np.uint8) & 0xF
        words = c[..., 0::2] | (c[..., 1::2] << 4)
    return np.ascontiguousarray(words), np.ascontiguousarray(byte.astype(np.uint8).reshape(k // 512, 16, n))


def unpack_weight(words, scales, fmt):
    g, p, n, _ = words.shape
    if fmt == "e4m3":
        vals = np.ascontiguousarray(words).view(ml_dtypes.float8_e4m3fn).astype(np.float64)
    else:
        nib = np.empty((g, p, n, 4), np.uint8)
        nib[..., 0::2] = words & 0xF
        nib[..., 1::2] = words >> 4
        vals = E2M1[nib]
    vals = vals * np.repeat(np.exp2(scales.astype(np.float64) - 127.0), 8, axis=1)[..., None]
    return vals.transpose(0, 1, 3, 2).reshape(g * 512, n)
def pack4(w):
    words, scales = pack_weight(w, "e2m1")
    return words.reshape(words.shape[0], 128, -1), scales


def unpack4(words, scales):
    return unpack_weight(words.reshape(words.shape[0], 128, -1, 2), scales, "e2m1")


def planes(Y):
    n, m = Y.shape
    b = f64(bf(Y)).reshape(n // 32, 32, m)
    amax = np.abs(b).max(1)
    byte = np.clip(np.where(amax > 0, np.frexp(amax)[1] - 1 + 127 - 7, 1), 1, 254)
    codes = (b * np.exp2(127.0 - byte)[:, None, :]).reshape(n, m).astype(np.float32).astype(ml_dtypes.float8_e4m3fn).view(np.uint8)
    words = codes.reshape(n // 512, 128, 4, m).transpose(0, 1, 3, 2)
    return np.ascontiguousarray(words), np.ascontiguousarray(byte.astype(np.uint8).reshape(n // 512, 16, m))


H, T, D, J, E = 8, 192, 512, 2048, 1024
R = H * T

def setup_inputs():
    s = mx_kscale(D)
    t = mx_kscale(J)
    Q = np.random.randn(D, R) * s[:, None]
    K = np.random.randn(D, J) / np.sqrt(D) / s[:, None]
    q_words, q_scales = pack_weight(Q, "e4m3")
    k_words, k_scales = pack4(K)
    key_weight = bf(np.exp(0.4 * np.random.randn(J)) * t)
    v = bf(np.random.randn(J, E) / np.sqrt(J) / t[:, None])
    u = bf(np.random.randn(H, T, E))
    out_gain = bf(np.exp(0.8 * np.random.randn(H, E)))
    return {"q_words": q_words, "q_scales": q_scales,
            "k_words": k_words, "k_scales": k_scales,
            "key_weight": key_weight, "v": v, "u": u, "out_gain": out_gain}

def reference(q_words, q_scales, k_words, k_scales, key_weight, v, u, out_gain):
    Q = unpack_weight(q_words, q_scales, "e4m3")
    K = unpack4(k_words, k_scales)
    S = Q.T @ K
    A = np.square(np.maximum(S, 0.0)) * f64(key_weight)[None, :]
    O = mxq(A, 1, "e4m3") @ mxq(f64(v), 0, "e4m3")
    gate = 1.0 / (1.0 + np.exp(-f64(u)))
    y = O.reshape(H, T, E) * f64(out_gain)[:, None, :] * gate
    Y = y.reshape(R, E).T
    words, scales = planes(Y)
    return y, words, scales

@@ -1,0 +1,438 @@
+from contextlib import ExitStack
+
+import concourse.mybir as mybir
+from concourse.masks import make_identity
+
+H, T, D, J, E = 8, 192, 512, 2048, 1024
+R = H * T
+FLOPS = 2 * R * J * D + 2 * R * J * E
+
+F32 = mybir.dt.float32
+BF16 = mybir.dt.bfloat16
+I32 = mybir.dt.int32
+U32 = mybir.dt.uint32
+U8 = mybir.dt.uint8
+FP8X4 = mybir.dt.float8_e4m3fn_x4
+FP4X4 = mybir.dt.float4_e2m1fn_x4
+ALU = mybir.AluOpType
+ACT = mybir.ActivationFunctionType
+
+P = 128
+PASSES = J // 512
+TILES = R // P
+HEAD_TILES = 4
+HALF = 512
+PLANE_BATCHES = (4, 4, 2, 1, 1)
+SMALLEST_NORMAL = 2.0 ** -126
+
+
+def tile_squared_relu_attention_h2_kernel(
+    tc, q_words, q_scales, k_words, k_scales, key_weight, v, u, out_gain, out_0, out_1, out_2
+):
+    nc = tc.nc
+    u_rows = u.rearrange("h i e -> (h i) e")
+    y_rows = out_0.rearrange("h i e -> (h i) e")
+    v_slots = v.rearrange("(q s r) e -> s q r e", s=16, r=8)
+    q_dram = q_words[0].rearrange("p n t -> p (n t)")
+
+    with ExitStack() as ctx:
+        keep = ctx.enter_context(tc.tile_pool(name="keep", bufs=1))
+        work = ctx.enter_context(tc.tile_pool(name="work", bufs=2))
+        psum = ctx.enter_context(tc.psum_pool(name="psum", bufs=1))
+        ctx.enter_context(tc.manual_schedule())
+
+        def kept(name, shape, dtype):
+            return keep.tile(shape, dtype, name=name, tag=name, align_bytes=64)
+
+        def rotating(tag, n, shape, dtype, bufs):
+            return work.tile(shape, dtype, name="%s_%d" % (tag, n), tag=tag, bufs=bufs, align_bytes=64)
+
+        def bank(tag, n, shape, dtype, bufs):
+            return psum.tile(shape, dtype, name="%s_%d" % (tag, n), tag=tag, bufs=bufs)
+
+        k_raw = kept("k_raw", [P, 2 * J], U8)
+        k_codes = kept("k_codes", [P, 2 * J], U8)
+        ks_raw = kept("ks_raw", [P, J], U8)
+        k_plane = kept("k_plane", [P, J], U8)
+        q_first = kept("q_first", [P, 512], U32)
+        q_rest = kept("q_rest", [P, R - 512], U32)
+        q_plane = kept("q_plane", [P, R], U8)
+        w_rows = kept("w_rows", [P, P], BF16)
+        ident_bf = kept("ident_bf", [P, P], BF16)
+        ident_f32 = kept("ident_f32", [P, P], F32)
+        halves = kept("halves", [P, 16], F32)
+
+        nc.vector.memset(w_rows[:], 0.0)
+        nc.vector.memset(ks_raw[:].bitcast(I32), 0)
+        nc.vector.memset(q_plane[:].bitcast(I32), 0)
+        make_identity(nc, ident_bf[:])
+        nc.gpsimd.memset(halves[:], 0.5)
+
+        nc.sync.dma_start(out=k_raw[:].bitcast(I32), in_=k_words[0].bitcast(I32))
+        nc.sync.dma_start(
+            out=w_rows[0:16, :].rearrange("s (q r) -> s q r", r=8),
+            in_=key_weight.rearrange("(q s r) -> s q r", s=16, r=8),
+        )
+        for quad in range(4):
+            nc.sync.dma_start(
+                out=ks_raw[32 * quad : 32 * quad + 4, :].bitcast(I32),
+                in_=k_scales[0, 4 * quad : 4 * quad + 4, :].bitcast(I32),
+            )
+        nc.sync.dma_start(out=q_first[:].bitcast(I32), in_=q_dram[:, 0:2048].bitcast(I32))
+        for quad in range(4):
+            nc.sync.dma_start(
+                out=q_plane[32 * quad : 32 * quad + 4, :].bitcast(I32),
+                in_=q_scales[0, 4 * quad : 4 * quad + 4, :].bitcast(I32),
+            )
+        u_tiles = {}
+
+        def load_u(first, count):
+            t_u = kept("u_%d" % first, [P, count, E], BF16)
+            nc.sync.dma_start(
+                out=t_u[:], in_=u_rows[first * P : (first + count) * P, :].rearrange("(n p) e -> p n e", p=P)
+            )
+            for n in range(count):
+                u_tiles[first + n] = t_u[:, n, :]
+
+        load_u(0, 1)
+        v_raw = []
+        for g in range(PASSES):
+            raw = rotating("v_raw", g, [P, 4, E], BF16, 4)
+            for t in range(4):
+                nc.sync.dma_start(out=raw[:, t, :], in_=v_slots[4 * g + t])
+            v_raw.append(raw)
+        nc.sync.dma_start(out=q_rest[:].bitcast(I32), in_=q_dram[:, 2048:].bitcast(I32))
+        load_u(1, 1)
+        gain_low = kept("gain_low", [P, 4, E], BF16)
+        nc.sync.dma_start(out=gain_low[:], in_=out_gain[0:4, :].partition_broadcast(P))
+        gain_mixed = kept("gain_mixed", [P, 4, E], BF16)
+        gain_pairs = out_gain.rearrange("(m two) e -> two m e", two=2)
+        for two in range(2):
+            nc.sync.dma_start(out=gain_mixed[64 * two : 64 * two + 64], in_=gain_pairs[two].partition_broadcast(64))
+        for first in range(2, TILES, 2):
+            load_u(first, 2)
+
+        nc.vector.tensor_copy(
+            out=k_codes[:].bitcast(I32).rearrange("p (s q w) -> p s q w", s=16, w=4),
+            in_=k_raw[:].bitcast(I32).rearrange("p (q s w) -> p s q w", s=16, w=4),
+        )
+        w_t = bank("turn", 0, [P, P], BF16, 1)
+        nc.tensor.transpose(w_t[:], w_rows[:], ident_bf[:])
+        w = w_t[:, 0:16]
+        minus_w = kept("minus_w", [P, 16], F32)
+        w_abs = kept("w_abs", [P, 16], F32)
+        w_neg = kept("w_neg", [P, 16], F32)
+        w_sign = kept("w_sign", [P, 16], F32)
+        guess = kept("guess", [P, 16], F32)
+        inverse = kept("inverse", [P, 16], F32)
+        quotient = kept("quotient", [P, 16], F32)
+        w_root = kept("w_root", [P, 16], F32)
+        nc.vector.tensor_scalar(minus_w[:], w, -1.0, SMALLEST_NORMAL, ALU.mult, ALU.max)
+        nc.vector.tensor_scalar(w_neg[:], w, 0.0, None, ALU.is_lt)
+        nc.vector.tensor_tensor(w_abs[:], minus_w[:], w, ALU.max)
+        nc.vector.scalar_tensor_tensor(w_sign[:], w, 0.0, w_neg[:], ALU.is_gt, ALU.subtract)
+        nc.gpsimd.tensor_tensor(guess[:], w_abs[:], halves[:], ALU.pow)
+        make_identity(nc, ident_f32[:])
+        nc.vector.tensor_copy(
+            out=k_plane[:].bitcast(I32).rearrange("p (s q w) -> p s q w", s=16, w=2),
+            in_=ks_raw[:].bitcast(I32).rearrange("p (q s w) -> p s q w", s=16, w=2),
+        )
+        nc.vector.reciprocal(inverse[:], guess[:])
+        nc.vector.scalar_tensor_tensor(quotient[:], w_abs[:], 0.5, inverse[:], ALU.mult, ALU.mult)
+        nc.vector.scalar_tensor_tensor(w_root[:], guess[:], 0.5, quotient[:], ALU.mult, ALU.add)
+
+        counts = {}
+
+        def nxt(tag):
+            counts[tag] = counts.get(tag, 0) + 1
+            return counts[tag]
+
+        def scores(out, slot, col0, width):
+            q_tile, c0 = (q_first, col0) if col0 < 512 else (q_rest, col0 - 512)
+            nc.tensor.matmul_mx(
+                out=out,
+                lhsT=k_codes[:, 256 * slot : 256 * slot + 256].bitcast(FP4X4),
+                lhsT_scale=k_plane[:, P * slot : P * slot + P],
+                rhs=q_tile[:, c0 : c0 + width].bitcast(FP8X4),
+                rhs_scale=q_plane[:, col0 : col0 + width],
+                start=True,
+                stop=True,
+            )
+
+        gates = {}
+
+        def sigmoid(i):
+            gates[i] = rotating("sigmoid", i, [P, E], F32, 3)
+            nc.scalar.activation(gates[i][:], u_tiles[i], ACT.Sigmoid)
+
+        gain_high = []
+
+        def gain_of(i):
+            pair, place = divmod(i, 3)
+            if place == 1:
+                return gain_mixed[:, pair, :]
+            head = 2 * pair + place // 2
+            return gain_low[:, head, :] if head < 4 else gain_high[0][:, head - 4, :]
+
+        factors = {}
+
+        def gate_times_gain(engine, i):
+            for h in range(2):
+                factors[i, h] = rotating("factor%d" % h, i, [P, HALF], F32, 1)
+                cols = slice(HALF * h, HALF * h + HALF)
+                engine.tensor_tensor(factors[i, h][:], gates[i][:, cols], gain_of(i)[:, cols], ALU.mult)
+
+        a_ops = {}
+
+        def quantize_a(grouped, places):
+            n = nxt("a_codes")
+            codes = rotating("a_codes", n, [P, 512], U32, 6)
+            plane = rotating("a_plane", n, [P, 512], U8, 6)
+            nc.vector.quantize_mx(out=codes[:].bitcast(FP8X4), scales=plane[:], in_=grouped[:])
+            for m, place in enumerate(places):
+                a_ops[place] = (codes[:, P * m : P * m + P], plane[:, P * m : P * m + P])
+
+        v_ops = {}
+        sums = {}
+
+        def value_pass(i, h, g):
+            if g == 0:
+                sums[i, h] = bank("sums", nxt("sums"), [P, HALF], F32, 4)
+            codes, plane = a_ops[i, g]
+            v_codes, v_plane = v_ops[g, h]
+            nc.tensor.matmul_mx(
+                out=sums[i, h][:],
+                lhsT=codes.bitcast(FP8X4),
+                lhsT_scale=plane,
+                rhs=v_codes[:].bitcast(FP8X4),
+                rhs_scale=v_plane[:],
+                start=(g == 0),
+                stop=(g == PASSES - 1),
+            )
+
+        def head_scores(g):
+            roots = rotating("roots", nxt("roots"), [P, 4, 512], F32, 2)
+            for t in range(4):
+                slot = 4 * g + t
+                s_bank = bank("scores", nxt("scores"), [P, 512], F32, 3)
+                scores(s_bank[:], slot, 0, 512)
+                nc.scalar.activation(roots[:, t, :], s_bank[:], ACT.Relu, scale=w_root[:, slot : slot + 1])
+            grouped = rotating("a_grouped", nxt("a_grouped"), [P, 2048], BF16, 2)
+            nc.scalar.activation(
+                grouped[:].rearrange("p (c i t) -> p c t i", i=4, t=4),
+                roots[:].rearrange("p t (c i) -> p c t i", i=4),
+                ACT.Square,
+            )
+            return grouped
+
+        def sign_v(g):
+            for t in range(4):
+                slot = 4 * g + t
+                nc.vector.tensor_scalar(
+                    v_raw[g][:, t, :], v_raw[g][:, t, :], w_sign[:, slot : slot + 1], None, ALU.mult
+                )
+
+        def quantize_v(g):
+            grouped = []
+            for h in range(2):
+                v_grouped = rotating("v_grouped", nxt("v_grouped"), [P, 2048], BF16, 3)
+                nc.vector.tensor_copy(
+                    out=v_grouped[:].rearrange("p (c i t) -> p c t i", i=4, t=4),
+                    in_=v_raw[g][:, :, HALF * h : HALF * h + HALF].rearrange("p t (c i) -> p c t i", i=4),
+                )
+                grouped.append(v_grouped)
+            for h in range(2):
+                codes = kept("v_codes_%d_%d" % (g, h), [P, HALF], U32)
+                plane = kept("v_plane_%d_%d" % (g, h), [P, HALF], U8)
+                nc.vector.quantize_mx(out=codes[:].bitcast(FP8X4), scales=plane[:], in_=grouped[h][:])
+                v_ops[g, h] = (codes, plane)
+
+        def unit_place(n):
+            pair, g = divmod(n, PASSES)
+            return HEAD_TILES + 2 * pair, g
+
+        score_banks = {}
+
+        def unit_scores(n, side):
+            first_tile, g = unit_place(n)
+            s_bank = bank("scores", nxt("scores"), [P, 2, 256], F32, 3)
+            for c in range(2):
+                scores(s_bank[:, c, :], 4 * g + 2 * side + c, first_tile * P, 256)
+            score_banks[n, side] = s_bank
+
+        unit_roots = {}
+
+        def unit_relu(n, side):
+            g = n % PASSES
+            if side == 0:
+                unit_roots[n] = rotating("roots", nxt("roots"), [P, 2, 256, 2], F32, 2)
+            slot = 4 * g + 2 * side
+            nc.vector.scalar_tensor_tensor(
+                unit_roots[n][:, side],
+                score_banks[n, side][:].rearrange("p c n -> p n c"),
+                0.0,
+                w_root[:, slot : slot + 2].unsqueeze(1).to_broadcast([P, 256, 2]),
+                ALU.max,
+                ALU.mult,
+            )
+
+        unit_grouped = {}
+
+        def unit_square(n):
+            if n % 2 == 0:
+                unit_grouped[n // 2] = rotating("a_grouped", nxt("a_grouped"), [P, 2048], BF16, 2)
+            part = unit_grouped[n // 2][:, 1024 * (n % 2) : 1024 * (n % 2) + 1024]
+            nc.scalar.activation(
+                part.rearrange("p (n s c) -> p n s c", s=2, c=2),
+                unit_roots[n][:].rearrange("p s n c -> p n s c"),
+                ACT.Square,
+            )
+
+        def unit_quantize(step):
+            places = []
+            for n in (2 * step, 2 * step + 1):
+                first_tile, g = unit_place(n)
+                places.extend([(first_tile, g), (first_tile + 1, g)])
+            quantize_a(unit_grouped[step], places)
+
+        sigmoid(0)
+        grouped_now = head_scores(0)
+        sign_v(0)
+        for g in range(PASSES):
+            quantize_v(g)
+            if g + 1 < PASSES:
+                sign_v(g + 1)
+                grouped_next = head_scores(g + 1)
+            quantize_a(grouped_now, [(i, g) for i in range(HEAD_TILES)])
+            if g + 1 < PASSES:
+                grouped_now = grouped_next
+            else:
+                unit_scores(0, 0)
+                unit_scores(0, 1)
+                unit_scores(1, 0)
+            for i in range(2):
+                for h in range(2):
+                    value_pass(i, h, g)
+        gain_high.append(rotating("v_raw", PASSES, [P, 4, E], BF16, 4))
+        nc.sync.dma_start(out=gain_high[0][:], in_=out_gain[4:8, :].partition_broadcast(P))
+        sigmoid(1)
+        sigmoid(2)
+        gate_times_gain(nc.vector, 0)
+
+        batch_of = {}
+        batches = []
+        first_tile = 0
+        for b, size in enumerate(PLANE_BATCHES):
+            for i in range(first_tile, first_tile + size):
+                batch_of[i] = (b, first_tile, size)
+            batches.append((b, first_tile, size))
+            first_tile += size
+        y_tiles = {}
+        y_sorted = {}
+        y_grouped = {}
+
+        def finish_y(i):
+            y_tiles[i] = rotating("y", i, [P, E], F32, 4)
+            for h in range(2):
+                nc.vector.tensor_tensor(
+                    y_tiles[i][:, HALF * h : HALF * h + HALF], sums[i, h][:], factors[i, h][:], ALU.mult
+                )
+            nc.sync.dma_start(out=y_rows[i * P : (i + 1) * P, :], in_=y_tiles[i][:])
+
+        def round_views(i, g):
+            if (i, g) not in y_sorted:
+                y_sorted[i, g] = rotating("y_sorted%d" % g, i, [P, HALF], BF16, 2)
+            return (
+                y_sorted[i, g][:].rearrange("r (s p c) -> r s p c", s=2, c=2),
+                y_tiles[i][:, HALF * g : HALF * g + HALF].rearrange("r (p s c) -> r s p c", s=2, c=2),
+            )
+
+        def turn_y(i):
+            b, first, size = batch_of[i]
+            turned = bank("turn", nxt("turn"), [P, 2, 2, P], F32, 1)
+            for g in range(2):
+                words = y_sorted[i, g][:].bitcast(F32)
+                for s in range(2):
+                    nc.tensor.transpose(turned[:, g, s, :], words[:, P * s : P * s + P], ident_f32[:])
+            if i == first:
+                y_grouped[b] = rotating("y_grouped", b, [P, 2, size * P * 4], BF16, 2)
+            place = i - first
+            nc.scalar.copy(
+                y_grouped[b][:, :, 512 * place : 512 * place + 512].bitcast(F32).rearrange("p g (r s) -> p g r s", s=2),
+                turned[:].rearrange("p g s r -> p g r s"),
+            )
+
+        plane_tiles = {}
+
+        def quantize_y(b, first, size, groups):
+            width = size * P
+            if b not in plane_tiles:
+                plane_tiles[b] = (
+                    kept("y_codes_%d" % b, [P, 2, width], U32),
+                    kept("y_plane_%d" % b, [P, 2, width], U8),
+                )
+            codes, plane = plane_tiles[b]
+            nc.vector.quantize_mx(
+                out=codes[:, groups].rearrange("p g n -> p (g n)").bitcast(FP8X4),
+                scales=plane[:, groups].rearrange("p g n -> p (g n)"),
+                in_=y_grouped[b][:, groups].rearrange("p g n -> p (g n)"),
+            )
+            if groups.stop == 2:
+                cols = slice(first * P, first * P + width)
+                nc.sync.dma_start(
+                    out=out_1[:, :, cols, :].rearrange("g p n t -> p g (n t)").bitcast(I32),
+                    in_=codes[:].bitcast(I32),
+                )
+                for quad in range(4):
+                    nc.sync.dma_start(
+                        out=out_2[:, 4 * quad : 4 * quad + 4, cols].rearrange("g q n -> q g n").bitcast(I32),
+                        in_=plane[32 * quad : 32 * quad + 4].bitcast(I32),
+                    )
+
+        unit_steps = (TILES - HEAD_TILES) // 2 * PASSES // 2
+        planes_due = {}
+        for b, first, size in batches:
+            step = first + size + 1
+            if size == 4:
+                planes_due[step] = (b, first, size, slice(0, 1))
+                planes_due[step + 1] = (b, first, size, slice(1, 2))
+            else:
+                planes_due[step] = (b, first, size, slice(0, 2))
+
+        for step in range(TILES + 2):
+            has_tile = step < TILES
+            has_units = step < unit_steps
+            if has_tile:
+                finish_y(step)
+            if step + 1 < TILES:
+                gate_times_gain(nc.gpsimd, step + 1)
+            if 1 <= step <= unit_steps:
+                unit_square(2 * step - 1)
+            if 1 <= step < TILES - 1:
+                for h in range(2):
+                    for g in range(PASSES):
+                        value_pass(step + 1, h, g)
+            if step + 3 < TILES:
+                sigmoid(step + 3)
+            if has_units:
+                unit_relu(2 * step, 0)
+                unit_scores(2 * step + 1, 1)
+                unit_relu(2 * step, 1)
+                unit_relu(2 * step + 1, 0)
+                unit_relu(2 * step + 1, 1)
+            if has_tile:
+                nc.scalar.copy(*round_views(step, 1))
+            if has_units:
+                unit_square(2 * step)
+            if 1 <= step <= TILES:
+                turn_y(step - 1)
+            if step + 1 < unit_steps:
+                unit_scores(2 * step + 2, 0)
+                unit_scores(2 * step + 2, 1)
+                unit_scores(2 * step + 3, 0)
+            if has_tile:
+                nc.vector.tensor_copy(*round_views(step, 0))
+            if 1 <= step <= unit_steps:
+                unit_quantize(step - 1)
+            if step in planes_due:
+                quantize_y(*planes_due[step])

@@ -22,7 +22,12 @@ PASSES = J // 512
 TILES = R // P
 HEAD_TILES = 4
 HALF = 512
-PLANE_BATCHES = (4, 4, 2, 1, 1)
+UNITS = (TILES - HEAD_TILES) // 2 * PASSES
+EARLY_V = 2
+HEAD_UNITS = 1
+UNIT_STEPS = 8
+LAST_GPSIMD_GATE = 8
+STORE_TILES = 4
 SMALLEST_NORMAL = 2.0 ** -126
 
 
@@ -62,29 +67,17 @@ def tile_squared_relu_attention_h2_kernel(
         ident_f32 = kept("ident_f32", [P, P], F32)
         halves = kept("halves", [P, 16], F32)
 
+        zeros = kept("zeros", [P, 16], F32)
         nc.vector.memset(w_rows[:], 0.0)
-        nc.vector.memset(ks_raw[:].bitcast(I32), 0)
+        nc.gpsimd.memset(zeros[:], 0.0)
+        nc.vector.memset(k_plane[:].bitcast(I32), 0)
         nc.vector.memset(q_plane[:].bitcast(I32), 0)
         make_identity(nc, ident_bf[:])
-        nc.gpsimd.memset(halves[:], 0.5)
+        make_identity(nc, ident_f32[:])
+        nc.scalar.activation(halves[:], zeros[:], ACT.Sigmoid)
 
-        nc.sync.dma_start(out=k_raw[:].bitcast(I32), in_=k_words[0].bitcast(I32))
-        nc.sync.dma_start(
-            out=w_rows[0:16, :].rearrange("s (q r) -> s q r", r=8),
-            in_=key_weight.rearrange("(q s r) -> s q r", s=16, r=8),
-        )
-        for quad in range(4):
-            nc.sync.dma_start(
-                out=ks_raw[32 * quad : 32 * quad + 4, :].bitcast(I32),
-                in_=k_scales[0, 4 * quad : 4 * quad + 4, :].bitcast(I32),
-            )
-        nc.sync.dma_start(out=q_first[:].bitcast(I32), in_=q_dram[:, 0:2048].bitcast(I32))
-        for quad in range(4):
-            nc.sync.dma_start(
-                out=q_plane[32 * quad : 32 * quad + 4, :].bitcast(I32),
-                in_=q_scales[0, 4 * quad : 4 * quad + 4, :].bitcast(I32),
-            )
         u_tiles = {}
+        v_raw = [rotating("v_raw", g, [P, 4, E], BF16, 4) for g in range(PASSES)]
 
         def load_u(first, count):
             t_u = kept("u_%d" % first, [P, count, E], BF16)
@@ -94,28 +87,62 @@ def tile_squared_relu_attention_h2_kernel(
             for n in range(count):
                 u_tiles[first + n] = t_u[:, n, :]
 
-        load_u(0, 1)
-        v_raw = []
-        for g in range(PASSES):
-            raw = rotating("v_raw", g, [P, 4, E], BF16, 4)
-            for t in range(4):
-                nc.sync.dma_start(out=raw[:, t, :], in_=v_slots[4 * g + t])
-            v_raw.append(raw)
+        def load_v(g, slots):
+            for t in slots:
+                nc.sync.dma_start(out=v_raw[g][:, t, :], in_=v_slots[4 * g + t])
+
+        def load_scale_rows(plane, rows, quads):
+            for quad in quads:
+                nc.sync.dma_start(
+                    out=plane[32 * quad : 32 * quad + 4, :].bitcast(I32),
+                    in_=rows[4 * quad : 4 * quad + 4, :].bitcast(I32),
+                )
+
+        gains = {}
+
+        def load_gains(pair, tile):
+            gains[pair] = tile
+            nc.sync.dma_start(out=tile[:, 0:3:2, :], in_=out_gain[2 * pair : 2 * pair + 2, :].partition_broadcast(P))
+            for two in range(2):
+                nc.sync.dma_start(
+                    out=tile[64 * two : 64 * two + 64, 1, :], in_=out_gain[2 * pair + two, :].partition_broadcast(64)
+                )
+
+        load_scale_rows(ks_raw, k_scales[0], range(4))
+        nc.sync.dma_start(
+            out=w_rows[0:16, :].rearrange("s (q r) -> s q r", r=8),
+            in_=key_weight.rearrange("(q s r) -> s q r", s=16, r=8),
+        )
+        nc.sync.dma_start(out=k_raw[:].bitcast(I32), in_=k_words[0].bitcast(I32))
+        load_v(0, range(EARLY_V))
+        nc.sync.dma_start(out=q_first[:].bitcast(I32), in_=q_dram[:, 0:2048].bitcast(I32))
+        load_scale_rows(q_plane, q_scales[0], range(4))
+        load_v(0, range(EARLY_V, 4))
+        for g in range(1, PASSES):
+            load_v(g, range(4))
+            if g == 1:
+                load_u(0, 1)
         nc.sync.dma_start(out=q_rest[:].bitcast(I32), in_=q_dram[:, 2048:].bitcast(I32))
         load_u(1, 1)
-        gain_low = kept("gain_low", [P, 4, E], BF16)
-        nc.sync.dma_start(out=gain_low[:], in_=out_gain[0:4, :].partition_broadcast(P))
-        gain_mixed = kept("gain_mixed", [P, 4, E], BF16)
-        gain_pairs = out_gain.rearrange("(m two) e -> two m e", two=2)
-        for two in range(2):
-            nc.sync.dma_start(out=gain_mixed[64 * two : 64 * two + 64], in_=gain_pairs[two].partition_broadcast(64))
-        for first in range(2, TILES, 2):
+        load_gains(0, kept("gains_0", [P, 3, E], BF16))
+        load_u(2, 2)
+        load_gains(1, kept("gains_1", [P, 3, E], BF16))
+        for first in range(4, TILES, 2):
             load_u(first, 2)
 
-        nc.vector.tensor_copy(
-            out=k_codes[:].bitcast(I32).rearrange("p (s q w) -> p s q w", s=16, w=4),
-            in_=k_raw[:].bitcast(I32).rearrange("p (q s w) -> p s q w", s=16, w=4),
-        )
+        def order_keys(ordered, raw, words, slots):
+            nc.vector.tensor_copy(
+                out=ordered.bitcast(I32).rearrange("p (s q w) -> p s q w", s=16, w=words)[:, slots],
+                in_=raw.bitcast(I32).rearrange("p (q s w) -> p s q w", s=16, w=words)[:, slots],
+            )
+
+        def order_key_scales(quads):
+            for quad in quads:
+                rows = slice(32 * quad, 32 * quad + 4)
+                order_keys(k_plane[rows, :], ks_raw[rows, :], 2, slice(0, 16))
+
+        order_key_scales(range(0, 1))
+
         w_t = bank("turn", 0, [P, P], BF16, 1)
         nc.tensor.transpose(w_t[:], w_rows[:], ident_bf[:])
         w = w_t[:, 0:16]
@@ -132,14 +159,23 @@ def tile_squared_relu_attention_h2_kernel(
         nc.vector.tensor_tensor(w_abs[:], minus_w[:], w, ALU.max)
         nc.vector.scalar_tensor_tensor(w_sign[:], w, 0.0, w_neg[:], ALU.is_gt, ALU.subtract)
         nc.gpsimd.tensor_tensor(guess[:], w_abs[:], halves[:], ALU.pow)
-        make_identity(nc, ident_f32[:])
-        nc.vector.tensor_copy(
-            out=k_plane[:].bitcast(I32).rearrange("p (s q w) -> p s q w", s=16, w=2),
-            in_=ks_raw[:].bitcast(I32).rearrange("p (q s w) -> p s q w", s=16, w=2),
-        )
+
+        def sign_v(g, slots):
+            for t in slots:
+                slot = 4 * g + t
+                nc.vector.tensor_scalar(
+                    v_raw[g][:, t, :], v_raw[g][:, t, :], w_sign[:, slot : slot + 1], None, ALU.mult
+                )
+
+        order_key_scales(range(1, 4))
+        order_keys(k_codes[:], k_raw[:], 4, slice(0, 4))
         nc.vector.reciprocal(inverse[:], guess[:])
+        sign_v(0, range(0, 1))
         nc.vector.scalar_tensor_tensor(quotient[:], w_abs[:], 0.5, inverse[:], ALU.mult, ALU.mult)
+        sign_v(0, range(1, 2))
         nc.vector.scalar_tensor_tensor(w_root[:], guess[:], 0.5, quotient[:], ALU.mult, ALU.add)
+        order_keys(k_codes[:], k_raw[:], 4, slice(4, 16))
+        sign_v(0, range(2, 4))
 
         counts = {}
 
@@ -165,29 +201,21 @@ def tile_squared_relu_attention_h2_kernel(
             gates[i] = rotating("sigmoid", i, [P, E], F32, 3)
             nc.scalar.activation(gates[i][:], u_tiles[i], ACT.Sigmoid)
 
-        gain_high = []
-
-        def gain_of(i):
-            pair, place = divmod(i, 3)
-            if place == 1:
-                return gain_mixed[:, pair, :]
-            head = 2 * pair + place // 2
-            return gain_low[:, head, :] if head < 4 else gain_high[0][:, head - 4, :]
-
         factors = {}
 
-        def gate_times_gain(engine, i):
-            for h in range(2):
-                factors[i, h] = rotating("factor%d" % h, i, [P, HALF], F32, 1)
-                cols = slice(HALF * h, HALF * h + HALF)
-                engine.tensor_tensor(factors[i, h][:], gates[i][:, cols], gain_of(i)[:, cols], ALU.mult)
+        def gate_times_gain(engine, i, h):
+            pair, place = divmod(i, 3)
+            factors[i, h] = rotating("factor%d" % h, i, [P, HALF], F32, 1)
+            cols = slice(HALF * h, HALF * h + HALF)
+            engine.tensor_tensor(factors[i, h][:], gates[i][:, cols], gains[pair][:, place, cols], ALU.mult)
 
         a_ops = {}
 
         def quantize_a(grouped, places):
             n = nxt("a_codes")
-            codes = rotating("a_codes", n, [P, 512], U32, 6)
-            plane = rotating("a_plane", n, [P, 512], U8, 6)
+            width = P * len(places)
+            codes = kept("a_codes_%d" % n, [P, width], U32)
+            plane = kept("a_plane_%d" % n, [P, width], U8)
             nc.vector.quantize_mx(out=codes[:].bitcast(FP8X4), scales=plane[:], in_=grouped[:])
             for m, place in enumerate(places):
                 a_ops[place] = (codes[:, P * m : P * m + P], plane[:, P * m : P * m + P])
@@ -217,20 +245,13 @@ def tile_squared_relu_attention_h2_kernel(
                 s_bank = bank("scores", nxt("scores"), [P, 512], F32, 3)
                 scores(s_bank[:], slot, 0, 512)
                 nc.scalar.activation(roots[:, t, :], s_bank[:], ACT.Relu, scale=w_root[:, slot : slot + 1])
-            grouped = rotating("a_grouped", nxt("a_grouped"), [P, 2048], BF16, 2)
+            grouped = rotating("a_grouped", nxt("a_grouped"), [P, 2048], BF16, 3)
             nc.scalar.activation(
                 grouped[:].rearrange("p (c i t) -> p c t i", i=4, t=4),
                 roots[:].rearrange("p t (c i) -> p c t i", i=4),
                 ACT.Square,
             )
             return grouped
-
-        def sign_v(g):
-            for t in range(4):
-                slot = 4 * g + t
-                nc.vector.tensor_scalar(
-                    v_raw[g][:, t, :], v_raw[g][:, t, :], w_sign[:, slot : slot + 1], None, ALU.mult
-                )
 
         def quantize_v(g):
             grouped = []
@@ -261,6 +282,7 @@ def tile_squared_relu_attention_h2_kernel(
             score_banks[n, side] = s_bank
 
         unit_roots = {}
+        unit_grouped = {}
 
         def unit_relu(n, side):
             g = n % PASSES
@@ -276,57 +298,69 @@ def tile_squared_relu_attention_h2_kernel(
                 ALU.mult,
             )
 
-        unit_grouped = {}
-
         def unit_square(n):
-            if n % 2 == 0:
-                unit_grouped[n // 2] = rotating("a_grouped", nxt("a_grouped"), [P, 2048], BF16, 2)
-            part = unit_grouped[n // 2][:, 1024 * (n % 2) : 1024 * (n % 2) + 1024]
+            unit_grouped[n] = rotating("a_grouped", nxt("a_grouped"), [P, 1024], BF16, 3)
             nc.scalar.activation(
-                part.rearrange("p (n s c) -> p n s c", s=2, c=2),
+                unit_grouped[n][:].rearrange("p (n s c) -> p n s c", s=2, c=2),
                 unit_roots[n][:].rearrange("p s n c -> p n s c"),
                 ACT.Square,
             )
 
-        def unit_quantize(step):
-            places = []
-            for n in (2 * step, 2 * step + 1):
-                first_tile, g = unit_place(n)
-                places.extend([(first_tile, g), (first_tile + 1, g)])
-            quantize_a(unit_grouped[step], places)
+        def unit_on_scalar(n):
+            g = n % PASSES
+            roots = rotating("roots", nxt("roots"), [P, 4, 256], F32, 2)
+            for side in range(2):
+                unit_scores(n, side)
+                for c in range(2):
+                    slot = 4 * g + 2 * side + c
+                    nc.scalar.activation(
+                        roots[:, 2 * side + c, :], score_banks[n, side][:, c, :], ACT.Relu, scale=w_root[:, slot : slot + 1]
+                    )
+            unit_grouped[n] = rotating("a_grouped", nxt("a_grouped"), [P, 1024], BF16, 3)
+            nc.scalar.activation(
+                unit_grouped[n][:].rearrange("p (c i t) -> p c t i", i=4, t=4),
+                roots[:].rearrange("p t (c i) -> p c t i", i=4),
+                ACT.Square,
+            )
 
-        sigmoid(0)
+        def unit_quantize(n):
+            first_tile, g = unit_place(n)
+            quantize_a(unit_grouped[n], [(first_tile, g), (first_tile + 1, g)])
+
+        vector_units = UNITS - HEAD_UNITS
+        units_of = {step: [] for step in range(-1, TILES + 3)}
+        for m in range(vector_units):
+            units_of[UNIT_STEPS - 1 - (vector_units - 1 - m) * UNIT_STEPS // vector_units].append(HEAD_UNITS + m)
+
+        def banks_of(step):
+            return [(n, side) for n in units_of[step] for side in range(2)]
+
         grouped_now = head_scores(0)
-        sign_v(0)
         for g in range(PASSES):
             quantize_v(g)
             if g + 1 < PASSES:
-                sign_v(g + 1)
+                sign_v(g + 1, range(4))
                 grouped_next = head_scores(g + 1)
             quantize_a(grouped_now, [(i, g) for i in range(HEAD_TILES)])
             if g + 1 < PASSES:
                 grouped_now = grouped_next
-            else:
-                unit_scores(0, 0)
-                unit_scores(0, 1)
-                unit_scores(1, 0)
+            if g == 2:
+                sigmoid(0)
+                sigmoid(1)
+                for n in range(HEAD_UNITS):
+                    unit_on_scalar(n)
+            if g == 3:
+                for n, side in banks_of(0)[:3]:
+                    unit_scores(n, side)
             for i in range(2):
                 for h in range(2):
                     value_pass(i, h, g)
-        gain_high.append(rotating("v_raw", PASSES, [P, 4, E], BF16, 4))
-        nc.sync.dma_start(out=gain_high[0][:], in_=out_gain[4:8, :].partition_broadcast(P))
-        sigmoid(1)
+        for pair in (2, 3):
+            load_gains(pair, rotating("v_raw", PASSES + pair, [P, 3, E], BF16, 4))
         sigmoid(2)
-        gate_times_gain(nc.vector, 0)
+        for h in range(2):
+            gate_times_gain(nc.vector, 0, h)
 
-        batch_of = {}
-        batches = []
-        first_tile = 0
-        for b, size in enumerate(PLANE_BATCHES):
-            for i in range(first_tile, first_tile + size):
-                batch_of[i] = (b, first_tile, size)
-            batches.append((b, first_tile, size))
-            first_tile += size
         y_tiles = {}
         y_sorted = {}
         y_grouped = {}
@@ -347,92 +381,123 @@ def tile_squared_relu_attention_h2_kernel(
                 y_tiles[i][:, HALF * g : HALF * g + HALF].rearrange("r (p s c) -> r s p c", s=2, c=2),
             )
 
-        def turn_y(i):
-            b, first, size = batch_of[i]
-            turned = bank("turn", nxt("turn"), [P, 2, 2, P], F32, 1)
-            for g in range(2):
+        def turn_y(i, groups, tag, bufs):
+            b, place = divmod(i, STORE_TILES)
+            count = len(groups)
+            turned = bank(tag, nxt(tag), [P, count, 2, P], F32, bufs)
+            for m, g in enumerate(groups):
                 words = y_sorted[i, g][:].bitcast(F32)
                 for s in range(2):
-                    nc.tensor.transpose(turned[:, g, s, :], words[:, P * s : P * s + P], ident_f32[:])
-            if i == first:
-                y_grouped[b] = rotating("y_grouped", b, [P, 2, size * P * 4], BF16, 2)
-            place = i - first
+                    nc.tensor.transpose(turned[:, m, s, :], words[:, P * s : P * s + P], ident_f32[:])
+            if b not in y_grouped:
+                y_grouped[b] = rotating("v_raw", 10 + b, [P, 2, STORE_TILES * P * 4], BF16, 4)
             nc.scalar.copy(
-                y_grouped[b][:, :, 512 * place : 512 * place + 512].bitcast(F32).rearrange("p g (r s) -> p g r s", s=2),
+                y_grouped[b][:, groups.start : groups.stop, 512 * place : 512 * place + 512]
+                .bitcast(F32)
+                .rearrange("p g (r s) -> p g r s", s=2),
                 turned[:].rearrange("p g s r -> p g r s"),
             )
 
         plane_tiles = {}
 
-        def quantize_y(b, first, size, groups):
-            width = size * P
+        def quantize_y(first, count, g):
+            b, place = divmod(first, STORE_TILES)
             if b not in plane_tiles:
                 plane_tiles[b] = (
-                    kept("y_codes_%d" % b, [P, 2, width], U32),
-                    kept("y_plane_%d" % b, [P, 2, width], U8),
+                    kept("y_codes_%d" % b, [P, 2, STORE_TILES * P], U32),
+                    kept("y_plane_%d" % b, [P, 2, STORE_TILES * P], U8),
                 )
             codes, plane = plane_tiles[b]
+            cols = slice(place * P, (place + count) * P)
             nc.vector.quantize_mx(
-                out=codes[:, groups].rearrange("p g n -> p (g n)").bitcast(FP8X4),
-                scales=plane[:, groups].rearrange("p g n -> p (g n)"),
-                in_=y_grouped[b][:, groups].rearrange("p g n -> p (g n)"),
+                out=codes[:, g, cols].bitcast(FP8X4),
+                scales=plane[:, g, cols],
+                in_=y_grouped[b][:, g, 4 * cols.start : 4 * cols.stop],
             )
-            if groups.stop == 2:
-                cols = slice(first * P, first * P + width)
+
+        def store_codes(first, count):
+            b, place = divmod(first, STORE_TILES)
+            nc.sync.dma_start(
+                out=out_1[:, :, first * P : (first + count) * P, :].rearrange("g p n t -> p g (n t)").bitcast(I32),
+                in_=plane_tiles[b][0][:, :, place * P : (place + count) * P].bitcast(I32),
+            )
+
+        def store_scales(b):
+            cols = slice(b * STORE_TILES * P, (b + 1) * STORE_TILES * P)
+            for quad in range(4):
                 nc.sync.dma_start(
-                    out=out_1[:, :, cols, :].rearrange("g p n t -> p g (n t)").bitcast(I32),
-                    in_=codes[:].bitcast(I32),
+                    out=out_2[:, 4 * quad : 4 * quad + 4, cols].rearrange("g q n -> q g n").bitcast(I32),
+                    in_=plane_tiles[b][1][32 * quad : 32 * quad + 4].bitcast(I32),
                 )
-                for quad in range(4):
-                    nc.sync.dma_start(
-                        out=out_2[:, 4 * quad : 4 * quad + 4, cols].rearrange("g q n -> q g n").bitcast(I32),
-                        in_=plane[32 * quad : 32 * quad + 4].bitcast(I32),
-                    )
 
-        unit_steps = (TILES - HEAD_TILES) // 2 * PASSES // 2
-        planes_due = {}
-        for b, first, size in batches:
-            step = first + size + 1
-            if size == 4:
-                planes_due[step] = (b, first, size, slice(0, 1))
-                planes_due[step + 1] = (b, first, size, slice(1, 2))
-            else:
-                planes_due[step] = (b, first, size, slice(0, 2))
-
-        for step in range(TILES + 2):
-            has_tile = step < TILES
-            has_units = step < unit_steps
-            if has_tile:
-                finish_y(step)
-            if step + 1 < TILES:
-                gate_times_gain(nc.gpsimd, step + 1)
-            if 1 <= step <= unit_steps:
-                unit_square(2 * step - 1)
-            if 1 <= step < TILES - 1:
+        last = TILES - 1
+        waiting = list(range(HEAD_UNITS))
+        for step in range(TILES):
+            units = units_of[step]
+            light = step >= UNIT_STEPS
+            finish_y(step)
+            if step < last:
+                for h in range(2):
+                    if step + 1 > LAST_GPSIMD_GATE:
+                        gate_times_gain(nc.vector, step + 1, h)
+                    elif h < len(units):
+                        gate_times_gain(nc.gpsimd, step + 1, h)
+            if units_of[step - 1] and not light:
+                unit_square(units_of[step - 1][-1])
+                waiting.append(units_of[step - 1][-1])
+            if 1 <= step < last:
                 for h in range(2):
                     for g in range(PASSES):
                         value_pass(step + 1, h, g)
             if step + 3 < TILES:
                 sigmoid(step + 3)
-            if has_units:
-                unit_relu(2 * step, 0)
-                unit_scores(2 * step + 1, 1)
-                unit_relu(2 * step, 1)
-                unit_relu(2 * step + 1, 0)
-                unit_relu(2 * step + 1, 1)
-            if has_tile:
-                nc.scalar.copy(*round_views(step, 1))
-            if has_units:
-                unit_square(2 * step)
-            if 1 <= step <= TILES:
-                turn_y(step - 1)
-            if step + 1 < unit_steps:
-                unit_scores(2 * step + 2, 0)
-                unit_scores(2 * step + 2, 1)
-                unit_scores(2 * step + 3, 0)
-            if has_tile:
+            for place, (n, side) in enumerate(banks_of(step)):
+                unit_relu(n, side)
+                if place == 0 and len(units) == 2:
+                    unit_scores(units[1], 1)
+            if step == last:
+                break
+            nc.scalar.copy(*round_views(step, 1))
+            if light:
+                nc.scalar.copy(*round_views(step, 0))
+            if len(units) == 2:
+                unit_square(units[0])
+            if step == UNIT_STEPS - 1:
+                unit_square(units[-1])
+            if step >= 1:
+                turn_y(step - 1, range(2), "turn", 1)
+            for n, side in banks_of(step + 1)[:3]:
+                unit_scores(n, side)
+            if not light:
                 nc.vector.tensor_copy(*round_views(step, 0))
-            if 1 <= step <= unit_steps:
-                unit_quantize(step - 1)
-            if step in planes_due:
-                quantize_y(*planes_due[step])
+            if len(units) == 1:
+                gate_times_gain(nc.vector, step + 1, 1)
+            for n in waiting:
+                unit_quantize(n)
+            waiting = units[:1] if len(units) == 2 else []
+            if step == UNIT_STEPS - 1:
+                for n in units:
+                    unit_quantize(n)
+                waiting = []
+            if step >= 3 and step % 2 == 1:
+                first = step - 3
+                for g in range(2):
+                    quantize_y(first, 2, g)
+                if first % STORE_TILES == 2:
+                    store_codes(first - 2, STORE_TILES)
+                    store_scales(first // STORE_TILES)
+
+        nc.scalar.copy(*round_views(last, 0))
+        turn_y(last - 1, range(2), "turn", 1)
+        nc.vector.tensor_copy(*round_views(last, 1))
+        turn_y(last, range(0, 1), "scores", 3)
+        turn_y(last, range(1, 2), "scores", 3)
+        for g in range(2):
+            quantize_y(last - 3, 2, g)
+        for g in range(2):
+            quantize_y(last - 1, 1, g)
+        store_codes(last - 3, 3)
+        for g in range(2):
+            quantize_y(last, 1, g)
+        store_codes(last, 1)
+        store_scales(last // STORE_TILES)

@@ -24,6 +24,7 @@ HEAD_TILES = 4
 HALF = 512
 UNITS = (TILES - HEAD_TILES) // 2 * PASSES
 EARLY_V = 2
+FIRST_V = 0
 HEAD_UNITS = 1
 UNIT_STEPS = 8
 LAST_GPSIMD_GATE = 8
@@ -73,8 +74,8 @@ def tile_squared_relu_attention_h2_kernel(
         nc.vector.memset(k_plane[:].bitcast(I32), 0)
         nc.vector.memset(q_plane[:].bitcast(I32), 0)
         make_identity(nc, ident_bf[:])
-        make_identity(nc, ident_f32[:])
         nc.scalar.activation(halves[:], zeros[:], ACT.Sigmoid)
+        nc.scalar.copy(ident_f32[:], ident_bf[:])
 
         u_tiles = {}
         v_raw = [rotating("v_raw", g, [P, 4, E], BF16, 4) for g in range(PASSES)]
@@ -113,8 +114,9 @@ def tile_squared_relu_attention_h2_kernel(
             out=w_rows[0:16, :].rearrange("s (q r) -> s q r", r=8),
             in_=key_weight.rearrange("(q s r) -> s q r", s=16, r=8),
         )
+        load_v(0, range(FIRST_V))
         nc.sync.dma_start(out=k_raw[:].bitcast(I32), in_=k_words[0].bitcast(I32))
-        load_v(0, range(EARLY_V))
+        load_v(0, range(FIRST_V, EARLY_V))
         nc.sync.dma_start(out=q_first[:].bitcast(I32), in_=q_dram[:, 0:2048].bitcast(I32))
         load_scale_rows(q_plane, q_scales[0], range(4))
         load_v(0, range(EARLY_V, 4))
@@ -126,9 +128,8 @@ def tile_squared_relu_attention_h2_kernel(
         load_u(1, 1)
         load_gains(0, kept("gains_0", [P, 3, E], BF16))
         load_u(2, 2)
+        load_u(4, 2)
         load_gains(1, kept("gains_1", [P, 3, E], BF16))
-        for first in range(4, TILES, 2):
-            load_u(first, 2)
 
         def order_keys(ordered, raw, words, slots):
             nc.vector.tensor_copy(
@@ -205,7 +206,10 @@ def tile_squared_relu_attention_h2_kernel(
 
         def gate_times_gain(engine, i, h):
             pair, place = divmod(i, 3)
-            factors[i, h] = rotating("factor%d" % h, i, [P, HALF], F32, 1)
+            if h == 0:
+                factors[i, h] = rotating("a_grouped", nxt("a_grouped"), [P, HALF], F32, 3)
+            else:
+                factors[i, h] = rotating("factor", i, [P, HALF], F32, 1)
             cols = slice(HALF * h, HALF * h + HALF)
             engine.tensor_tensor(factors[i, h][:], gates[i][:, cols], gains[pair][:, place, cols], ALU.mult)
 
@@ -232,8 +236,8 @@ def tile_squared_relu_attention_h2_kernel(
                 out=sums[i, h][:],
                 lhsT=codes.bitcast(FP8X4),
                 lhsT_scale=plane,
-                rhs=v_codes[:].bitcast(FP8X4),
-                rhs_scale=v_plane[:],
+                rhs=v_codes.bitcast(FP8X4),
+                rhs_scale=v_plane,
                 start=(g == 0),
                 stop=(g == PASSES - 1),
             )
@@ -253,20 +257,20 @@ def tile_squared_relu_attention_h2_kernel(
             )
             return grouped
 
-        def quantize_v(g):
-            grouped = []
+        def group_v(g):
+            v_grouped = rotating("v_grouped", g, [P, 4 * E], BF16, 2)
+            nc.vector.tensor_copy(
+                out=v_grouped[:].rearrange("p (c i t) -> p c t i", i=4, t=4),
+                in_=v_raw[g][:].rearrange("p t (c i) -> p c t i", i=4),
+            )
+            return v_grouped
+
+        def quantize_v(g, v_grouped):
+            codes = kept("v_codes_%d" % g, [P, E], U32)
+            plane = kept("v_plane_%d" % g, [P, E], U8)
+            nc.vector.quantize_mx(out=codes[:].bitcast(FP8X4), scales=plane[:], in_=v_grouped[:])
             for h in range(2):
-                v_grouped = rotating("v_grouped", nxt("v_grouped"), [P, 2048], BF16, 3)
-                nc.vector.tensor_copy(
-                    out=v_grouped[:].rearrange("p (c i t) -> p c t i", i=4, t=4),
-                    in_=v_raw[g][:, :, HALF * h : HALF * h + HALF].rearrange("p t (c i) -> p c t i", i=4),
-                )
-                grouped.append(v_grouped)
-            for h in range(2):
-                codes = kept("v_codes_%d_%d" % (g, h), [P, HALF], U32)
-                plane = kept("v_plane_%d_%d" % (g, h), [P, HALF], U8)
-                nc.vector.quantize_mx(out=codes[:].bitcast(FP8X4), scales=plane[:], in_=grouped[h][:])
-                v_ops[g, h] = (codes, plane)
+                v_ops[g, h] = (codes[:, HALF * h : HALF * h + HALF], plane[:, HALF * h : HALF * h + HALF])
 
         def unit_place(n):
             pair, g = divmod(n, PASSES)
@@ -298,10 +302,15 @@ def tile_squared_relu_attention_h2_kernel(
                 ALU.mult,
             )
 
+        def grouped_part(n):
+            step, place = divmod(n, 2)
+            if place == 0:
+                unit_grouped[step] = rotating("a_grouped", nxt("a_grouped"), [P, 2048], BF16, 3)
+            return unit_grouped[step][:, 1024 * place : 1024 * place + 1024]
+
         def unit_square(n):
-            unit_grouped[n] = rotating("a_grouped", nxt("a_grouped"), [P, 1024], BF16, 3)
             nc.scalar.activation(
-                unit_grouped[n][:].rearrange("p (n s c) -> p n s c", s=2, c=2),
+                grouped_part(n).rearrange("p (n s c) -> p n s c", s=2, c=2),
                 unit_roots[n][:].rearrange("p s n c -> p n s c"),
                 ACT.Square,
             )
@@ -316,32 +325,34 @@ def tile_squared_relu_attention_h2_kernel(
                     nc.scalar.activation(
                         roots[:, 2 * side + c, :], score_banks[n, side][:, c, :], ACT.Relu, scale=w_root[:, slot : slot + 1]
                     )
-            unit_grouped[n] = rotating("a_grouped", nxt("a_grouped"), [P, 1024], BF16, 3)
             nc.scalar.activation(
-                unit_grouped[n][:].rearrange("p (c i t) -> p c t i", i=4, t=4),
+                grouped_part(n).rearrange("p (c i t) -> p c t i", i=4, t=4),
                 roots[:].rearrange("p t (c i) -> p c t i", i=4),
                 ACT.Square,
             )
 
-        def unit_quantize(n):
-            first_tile, g = unit_place(n)
-            quantize_a(unit_grouped[n], [(first_tile, g), (first_tile + 1, g)])
+        def quantize_units(step):
+            first_tile, g = unit_place(2 * step)
+            quantize_a(unit_grouped[step], [(first_tile + m, g + place) for place in range(2) for m in range(2)])
 
-        vector_units = UNITS - HEAD_UNITS
         units_of = {step: [] for step in range(-1, TILES + 3)}
-        for m in range(vector_units):
-            units_of[UNIT_STEPS - 1 - (vector_units - 1 - m) * UNIT_STEPS // vector_units].append(HEAD_UNITS + m)
+        for n in range(HEAD_UNITS, UNITS):
+            units_of[n // 2].append(n)
 
         def banks_of(step):
             return [(n, side) for n in units_of[step] for side in range(2)]
 
         grouped_now = head_scores(0)
         for g in range(PASSES):
-            quantize_v(g)
+            v_grouped = group_v(g)
             if g + 1 < PASSES:
                 sign_v(g + 1, range(4))
                 grouped_next = head_scores(g + 1)
-            quantize_a(grouped_now, [(i, g) for i in range(HEAD_TILES)])
+                quantize_v(g, v_grouped)
+                quantize_a(grouped_now, [(i, g) for i in range(HEAD_TILES)])
+            else:
+                quantize_a(grouped_now, [(i, g) for i in range(HEAD_TILES)])
+                quantize_v(g, v_grouped)
             if g + 1 < PASSES:
                 grouped_now = grouped_next
             if g == 2:
@@ -355,8 +366,6 @@ def tile_squared_relu_attention_h2_kernel(
             for i in range(2):
                 for h in range(2):
                     value_pass(i, h, g)
-        for pair in (2, 3):
-            load_gains(pair, rotating("v_raw", PASSES + pair, [P, 3, E], BF16, 4))
         sigmoid(2)
         for h in range(2):
             gate_times_gain(nc.vector, 0, h)
@@ -431,20 +440,25 @@ def tile_squared_relu_attention_h2_kernel(
                 )
 
         last = TILES - 1
-        waiting = list(range(HEAD_UNITS))
         for step in range(TILES):
             units = units_of[step]
             light = step >= UNIT_STEPS
+            on_gpsimd = step + 1 <= LAST_GPSIMD_GATE
+            if on_gpsimd:
+                gate_times_gain(nc.gpsimd, step + 1, 0)
             finish_y(step)
-            if step < last:
+            if step % 2 == 0 and step + 6 < TILES:
+                load_u(step + 6, 2)
+            if step % 3 == 1 and step + 5 < TILES:
+                pair = (step + 5) // 3
+                load_gains(pair, rotating("v_raw", PASSES + pair, [P, 3, E], BF16, 4))
+            if on_gpsimd:
+                gate_times_gain(nc.gpsimd, step + 1, 1)
+            elif step < last:
                 for h in range(2):
-                    if step + 1 > LAST_GPSIMD_GATE:
-                        gate_times_gain(nc.vector, step + 1, h)
-                    elif h < len(units):
-                        gate_times_gain(nc.gpsimd, step + 1, h)
+                    gate_times_gain(nc.vector, step + 1, h)
             if units_of[step - 1] and not light:
                 unit_square(units_of[step - 1][-1])
-                waiting.append(units_of[step - 1][-1])
             if 1 <= step < last:
                 for h in range(2):
                     for g in range(PASSES):
@@ -470,22 +484,16 @@ def tile_squared_relu_attention_h2_kernel(
                 unit_scores(n, side)
             if not light:
                 nc.vector.tensor_copy(*round_views(step, 0))
-            if len(units) == 1:
-                gate_times_gain(nc.vector, step + 1, 1)
-            for n in waiting:
-                unit_quantize(n)
-            waiting = units[:1] if len(units) == 2 else []
+            if step in (5, 6, 9, 10):
+                b, g = divmod(step - 5, STORE_TILES)
+                quantize_y(b * STORE_TILES, STORE_TILES, g)
+                if g == 1:
+                    store_codes(b * STORE_TILES, STORE_TILES)
+                    store_scales(b)
+            if 1 <= step < UNIT_STEPS:
+                quantize_units(step - 1)
             if step == UNIT_STEPS - 1:
-                for n in units:
-                    unit_quantize(n)
-                waiting = []
-            if step >= 3 and step % 2 == 1:
-                first = step - 3
-                for g in range(2):
-                    quantize_y(first, 2, g)
-                if first % STORE_TILES == 2:
-                    store_codes(first - 2, STORE_TILES)
-                    store_scales(first // STORE_TILES)
+                quantize_units(step)
 
         nc.scalar.copy(*round_views(last, 0))
         turn_y(last - 1, range(2), "turn", 1)

from contextlib import ExitStack

import concourse.mybir as mybir
from concourse.masks import make_identity

H, T, D, J, E = 8, 192, 512, 2048, 1024
R = H * T
FLOPS = 2 * R * J * D + 2 * R * J * E

F32 = mybir.dt.float32
BF16 = mybir.dt.bfloat16
I32 = mybir.dt.int32
U32 = mybir.dt.uint32
U8 = mybir.dt.uint8
FP8X4 = mybir.dt.float8_e4m3fn_x4
FP4X4 = mybir.dt.float4_e2m1fn_x4
ALU = mybir.AluOpType
ACT = mybir.ActivationFunctionType

P = 128
PASSES = J // 512
TILES = R // P
HEAD_TILES = 4
HALF = 512
UNITS = (TILES - HEAD_TILES) // 2 * PASSES
EARLY_V = 2
FIRST_V = 0
HEAD_UNITS = 1
UNIT_STEPS = 8
LAST_GPSIMD_GATE = 8
STORE_TILES = 4
SMALLEST_NORMAL = 2.0 ** -126


def tile_squared_relu_attention_h2_kernel(
    tc, q_words, q_scales, k_words, k_scales, key_weight, v, u, out_gain, out_0, out_1, out_2
):
    nc = tc.nc
    u_rows = u.rearrange("h i e -> (h i) e")
    y_rows = out_0.rearrange("h i e -> (h i) e")
    v_slots = v.rearrange("(q s r) e -> s q r e", s=16, r=8)
    q_dram = q_words[0].rearrange("p n t -> p (n t)")

    with ExitStack() as ctx:
        keep = ctx.enter_context(tc.tile_pool(name="keep", bufs=1))
        work = ctx.enter_context(tc.tile_pool(name="work", bufs=2))
        psum = ctx.enter_context(tc.psum_pool(name="psum", bufs=1))
        ctx.enter_context(tc.manual_schedule())

        def kept(name, shape, dtype):
            return keep.tile(shape, dtype, name=name, tag=name, align_bytes=64)

        def rotating(tag, n, shape, dtype, bufs):
            return work.tile(shape, dtype, name="%s_%d" % (tag, n), tag=tag, bufs=bufs, align_bytes=64)

        def bank(tag, n, shape, dtype, bufs):
            return psum.tile(shape, dtype, name="%s_%d" % (tag, n), tag=tag, bufs=bufs)

        k_raw = kept("k_raw", [P, 2 * J], U8)
        k_codes = kept("k_codes", [P, 2 * J], U8)
        ks_raw = kept("ks_raw", [P, J], U8)
        k_plane = kept("k_plane", [P, J], U8)
        q_first = kept("q_first", [P, 512], U32)
        q_rest = kept("q_rest", [P, R - 512], U32)
        q_plane = kept("q_plane", [P, R], U8)
        w_rows = kept("w_rows", [P, P], BF16)
        ident_bf = kept("ident_bf", [P, P], BF16)
        ident_f32 = kept("ident_f32", [P, P], F32)
        halves = kept("halves", [P, 16], F32)

        zeros = kept("zeros", [P, 16], F32)
        nc.vector.memset(w_rows[:], 0.0)
        nc.gpsimd.memset(zeros[:], 0.0)
        nc.vector.memset(k_plane[:].bitcast(I32), 0)
        nc.vector.memset(q_plane[:].bitcast(I32), 0)
        make_identity(nc, ident_bf[:])
        nc.scalar.activation(halves[:], zeros[:], ACT.Sigmoid)
        nc.scalar.copy(ident_f32[:], ident_bf[:])

        u_tiles = {}
        v_raw = [rotating("v_raw", g, [P, 4, E], BF16, 4) for g in range(PASSES)]

        def load_u(first, count):
            t_u = kept("u_%d" % first, [P, count, E], BF16)
            nc.sync.dma_start(
                out=t_u[:], in_=u_rows[first * P : (first + count) * P, :].rearrange("(n p) e -> p n e", p=P)
            )
            for n in range(count):
                u_tiles[first + n] = t_u[:, n, :]

        def load_v(g, slots):
            for t in slots:
                nc.sync.dma_start(out=v_raw[g][:, t, :], in_=v_slots[4 * g + t])

        def load_scale_rows(plane, rows, quads):
            for quad in quads:
                nc.sync.dma_start(
                    out=plane[32 * quad : 32 * quad + 4, :].bitcast(I32),
                    in_=rows[4 * quad : 4 * quad + 4, :].bitcast(I32),
                )

        gains = {}

        def load_gains(pair, tile):
            gains[pair] = tile
            nc.sync.dma_start(out=tile[:, 0:3:2, :], in_=out_gain[2 * pair : 2 * pair + 2, :].partition_broadcast(P))
            for two in range(2):
                nc.sync.dma_start(
                    out=tile[64 * two : 64 * two + 64, 1, :], in_=out_gain[2 * pair + two, :].partition_broadcast(64)
                )

        load_scale_rows(ks_raw, k_scales[0], range(4))
        nc.sync.dma_start(
            out=w_rows[0:16, :].rearrange("s (q r) -> s q r", r=8),
            in_=key_weight.rearrange("(q s r) -> s q r", s=16, r=8),
        )
        load_v(0, range(FIRST_V))
        nc.sync.dma_start(out=k_raw[:].bitcast(I32), in_=k_words[0].bitcast(I32))
        load_v(0, range(FIRST_V, EARLY_V))
        nc.sync.dma_start(out=q_first[:].bitcast(I32), in_=q_dram[:, 0:2048].bitcast(I32))
        load_scale_rows(q_plane, q_scales[0], range(4))
        load_v(0, range(EARLY_V, 4))
        for g in range(1, PASSES):
            load_v(g, range(4))
            if g == 1:
                load_u(0, 1)
        nc.sync.dma_start(out=q_rest[:].bitcast(I32), in_=q_dram[:, 2048:].bitcast(I32))
        load_u(1, 1)
        load_gains(0, kept("gains_0", [P, 3, E], BF16))
        load_u(2, 2)
        load_u(4, 2)
        load_gains(1, kept("gains_1", [P, 3, E], BF16))

        def order_keys(ordered, raw, words, slots):
            nc.vector.tensor_copy(
                out=ordered.bitcast(I32).rearrange("p (s q w) -> p s q w", s=16, w=words)[:, slots],
                in_=raw.bitcast(I32).rearrange("p (q s w) -> p s q w", s=16, w=words)[:, slots],
            )

        def order_key_scales(quads):
            for quad in quads:
                rows = slice(32 * quad, 32 * quad + 4)
                order_keys(k_plane[rows, :], ks_raw[rows, :], 2, slice(0, 16))

        order_key_scales(range(0, 1))

        w_t = bank("turn", 0, [P, P], BF16, 1)
        nc.tensor.transpose(w_t[:], w_rows[:], ident_bf[:])
        w = w_t[:, 0:16]
        minus_w = kept("minus_w", [P, 16], F32)
        w_abs = kept("w_abs", [P, 16], F32)
        w_neg = kept("w_neg", [P, 16], F32)
        w_sign = kept("w_sign", [P, 16], F32)
        guess = kept("guess", [P, 16], F32)
        inverse = kept("inverse", [P, 16], F32)
        quotient = kept("quotient", [P, 16], F32)
        w_root = kept("w_root", [P, 16], F32)
        nc.vector.tensor_scalar(minus_w[:], w, -1.0, SMALLEST_NORMAL, ALU.mult, ALU.max)
        nc.vector.tensor_scalar(w_neg[:], w, 0.0, None, ALU.is_lt)
        nc.vector.tensor_tensor(w_abs[:], minus_w[:], w, ALU.max)
        nc.vector.scalar_tensor_tensor(w_sign[:], w, 0.0, w_neg[:], ALU.is_gt, ALU.subtract)
        nc.gpsimd.tensor_tensor(guess[:], w_abs[:], halves[:], ALU.pow)

        def sign_v(g, slots):
            for t in slots:
                slot = 4 * g + t
                nc.vector.tensor_scalar(
                    v_raw[g][:, t, :], v_raw[g][:, t, :], w_sign[:, slot : slot + 1], None, ALU.mult
                )

        order_key_scales(range(1, 4))
        order_keys(k_codes[:], k_raw[:], 4, slice(0, 4))
        nc.vector.reciprocal(inverse[:], guess[:])
        sign_v(0, range(0, 1))
        nc.vector.scalar_tensor_tensor(quotient[:], w_abs[:], 0.5, inverse[:], ALU.mult, ALU.mult)
        sign_v(0, range(1, 2))
        nc.vector.scalar_tensor_tensor(w_root[:], guess[:], 0.5, quotient[:], ALU.mult, ALU.add)
        order_keys(k_codes[:], k_raw[:], 4, slice(4, 16))
        sign_v(0, range(2, 4))

        counts = {}

        def nxt(tag):
            counts[tag] = counts.get(tag, 0) + 1
            return counts[tag]

        def scores(out, slot, col0, width):
            q_tile, c0 = (q_first, col0) if col0 < 512 else (q_rest, col0 - 512)
            nc.tensor.matmul_mx(
                out=out,
                lhsT=k_codes[:, 256 * slot : 256 * slot + 256].bitcast(FP4X4),
                lhsT_scale=k_plane[:, P * slot : P * slot + P],
                rhs=q_tile[:, c0 : c0 + width].bitcast(FP8X4),
                rhs_scale=q_plane[:, col0 : col0 + width],
                start=True,
                stop=True,
            )

        gates = {}

        def sigmoid(i):
            gates[i] = rotating("sigmoid", i, [P, E], F32, 3)
            nc.scalar.activation(gates[i][:], u_tiles[i], ACT.Sigmoid)

        factors = {}

        def gate_times_gain(engine, i, h):
            pair, place = divmod(i, 3)
            if h == 0:
                factors[i, h] = rotating("a_grouped", nxt("a_grouped"), [P, HALF], F32, 3)
            else:
                factors[i, h] = rotating("factor", i, [P, HALF], F32, 1)
            cols = slice(HALF * h, HALF * h + HALF)
            engine.tensor_tensor(factors[i, h][:], gates[i][:, cols], gains[pair][:, place, cols], ALU.mult)

        a_ops = {}

        def quantize_a(grouped, places):
            n = nxt("a_codes")
            width = P * len(places)
            codes = kept("a_codes_%d" % n, [P, width], U32)
            plane = kept("a_plane_%d" % n, [P, width], U8)
            nc.vector.quantize_mx(out=codes[:].bitcast(FP8X4), scales=plane[:], in_=grouped[:])
            for m, place in enumerate(places):
                a_ops[place] = (codes[:, P * m : P * m + P], plane[:, P * m : P * m + P])

        v_ops = {}
        sums = {}

        def value_pass(i, h, g):
            if g == 0:
                sums[i, h] = bank("sums", nxt("sums"), [P, HALF], F32, 4)
            codes, plane = a_ops[i, g]
            v_codes, v_plane = v_ops[g, h]
            nc.tensor.matmul_mx(
                out=sums[i, h][:],
                lhsT=codes.bitcast(FP8X4),
                lhsT_scale=plane,
                rhs=v_codes.bitcast(FP8X4),
                rhs_scale=v_plane,
                start=(g == 0),
                stop=(g == PASSES - 1),
            )

        def head_scores(g):
            roots = rotating("roots", nxt("roots"), [P, 4, 512], F32, 2)
            for t in range(4):
                slot = 4 * g + t
                s_bank = bank("scores", nxt("scores"), [P, 512], F32, 3)
                scores(s_bank[:], slot, 0, 512)
                nc.scalar.activation(roots[:, t, :], s_bank[:], ACT.Relu, scale=w_root[:, slot : slot + 1])
            grouped = rotating("a_grouped", nxt("a_grouped"), [P, 2048], BF16, 3)
            nc.scalar.activation(
                grouped[:].rearrange("p (c i t) -> p c t i", i=4, t=4),
                roots[:].rearrange("p t (c i) -> p c t i", i=4),
                ACT.Square,
            )
            return grouped

        def group_v(g):
            v_grouped = rotating("v_grouped", g, [P, 4 * E], BF16, 2)
            nc.vector.tensor_copy(
                out=v_grouped[:].rearrange("p (c i t) -> p c t i", i=4, t=4),
                in_=v_raw[g][:].rearrange("p t (c i) -> p c t i", i=4),
            )
            return v_grouped

        def quantize_v(g, v_grouped):
            codes = kept("v_codes_%d" % g, [P, E], U32)
            plane = kept("v_plane_%d" % g, [P, E], U8)
            nc.vector.quantize_mx(out=codes[:].bitcast(FP8X4), scales=plane[:], in_=v_grouped[:])
            for h in range(2):
                v_ops[g, h] = (codes[:, HALF * h : HALF * h + HALF], plane[:, HALF * h : HALF * h + HALF])

        def unit_place(n):
            pair, g = divmod(n, PASSES)
            return HEAD_TILES + 2 * pair, g

        score_banks = {}

        def unit_scores(n, side):
            first_tile, g = unit_place(n)
            s_bank = bank("scores", nxt("scores"), [P, 2, 256], F32, 3)
            for c in range(2):
                scores(s_bank[:, c, :], 4 * g + 2 * side + c, first_tile * P, 256)
            score_banks[n, side] = s_bank

        unit_roots = {}
        unit_grouped = {}

        def unit_relu(n, side):
            g = n % PASSES
            if side == 0:
                unit_roots[n] = rotating("roots", nxt("roots"), [P, 2, 256, 2], F32, 2)
            slot = 4 * g + 2 * side
            nc.vector.scalar_tensor_tensor(
                unit_roots[n][:, side],
                score_banks[n, side][:].rearrange("p c n -> p n c"),
                0.0,
                w_root[:, slot : slot + 2].unsqueeze(1).to_broadcast([P, 256, 2]),
                ALU.max,
                ALU.mult,
            )

        def grouped_part(n):
            step, place = divmod(n, 2)
            if place == 0:
                unit_grouped[step] = rotating("a_grouped", nxt("a_grouped"), [P, 2048], BF16, 3)
            return unit_grouped[step][:, 1024 * place : 1024 * place + 1024]

        def unit_square(n):
            nc.scalar.activation(
                grouped_part(n).rearrange("p (n s c) -> p n s c", s=2, c=2),
                unit_roots[n][:].rearrange("p s n c -> p n s c"),
                ACT.Square,
            )

        def unit_on_scalar(n):
            g = n % PASSES
            roots = rotating("roots", nxt("roots"), [P, 4, 256], F32, 2)
            for side in range(2):
                unit_scores(n, side)
                for c in range(2):
                    slot = 4 * g + 2 * side + c
                    nc.scalar.activation(
                        roots[:, 2 * side + c, :], score_banks[n, side][:, c, :], ACT.Relu, scale=w_root[:, slot : slot + 1]
                    )
            nc.scalar.activation(
                grouped_part(n).rearrange("p (c i t) -> p c t i", i=4, t=4),
                roots[:].rearrange("p t (c i) -> p c t i", i=4),
                ACT.Square,
            )

        def quantize_units(step):
            first_tile, g = unit_place(2 * step)
            quantize_a(unit_grouped[step], [(first_tile + m, g + place) for place in range(2) for m in range(2)])

        units_of = {step: [] for step in range(-1, TILES + 3)}
        for n in range(HEAD_UNITS, UNITS):
            units_of[n // 2].append(n)

        def banks_of(step):
            return [(n, side) for n in units_of[step] for side in range(2)]

        grouped_now = head_scores(0)
        for g in range(PASSES):
            v_grouped = group_v(g)
            if g + 1 < PASSES:
                sign_v(g + 1, range(4))
                grouped_next = head_scores(g + 1)
                quantize_v(g, v_grouped)
                quantize_a(grouped_now, [(i, g) for i in range(HEAD_TILES)])
            else:
                quantize_a(grouped_now, [(i, g) for i in range(HEAD_TILES)])
                quantize_v(g, v_grouped)
            if g + 1 < PASSES:
                grouped_now = grouped_next
            if g == 2:
                sigmoid(0)
                sigmoid(1)
                for n in range(HEAD_UNITS):
                    unit_on_scalar(n)
            if g == 3:
                for n, side in banks_of(0)[:3]:
                    unit_scores(n, side)
            for i in range(2):
                for h in range(2):
                    value_pass(i, h, g)
        sigmoid(2)
        for h in range(2):
            gate_times_gain(nc.vector, 0, h)

        y_tiles = {}
        y_sorted = {}
        y_grouped = {}

        def finish_y(i):
            y_tiles[i] = rotating("y", i, [P, E], F32, 4)
            for h in range(2):
                nc.vector.tensor_tensor(
                    y_tiles[i][:, HALF * h : HALF * h + HALF], sums[i, h][:], factors[i, h][:], ALU.mult
                )
            nc.sync.dma_start(out=y_rows[i * P : (i + 1) * P, :], in_=y_tiles[i][:])

        def round_views(i, g):
            if (i, g) not in y_sorted:
                y_sorted[i, g] = rotating("y_sorted%d" % g, i, [P, HALF], BF16, 2)
            return (
                y_sorted[i, g][:].rearrange("r (s p c) -> r s p c", s=2, c=2),
                y_tiles[i][:, HALF * g : HALF * g + HALF].rearrange("r (p s c) -> r s p c", s=2, c=2),
            )

        def turn_y(i, groups, tag, bufs):
            b, place = divmod(i, STORE_TILES)
            count = len(groups)
            turned = bank(tag, nxt(tag), [P, count, 2, P], F32, bufs)
            for m, g in enumerate(groups):
                words = y_sorted[i, g][:].bitcast(F32)
                for s in range(2):
                    nc.tensor.transpose(turned[:, m, s, :], words[:, P * s : P * s + P], ident_f32[:])
            if b not in y_grouped:
                y_grouped[b] = rotating("v_raw", 10 + b, [P, 2, STORE_TILES * P * 4], BF16, 4)
            nc.scalar.copy(
                y_grouped[b][:, groups.start : groups.stop, 512 * place : 512 * place + 512]
                .bitcast(F32)
                .rearrange("p g (r s) -> p g r s", s=2),
                turned[:].rearrange("p g s r -> p g r s"),
            )

        plane_tiles = {}

        def quantize_y(first, count, g):
            b, place = divmod(first, STORE_TILES)
            if b not in plane_tiles:
                plane_tiles[b] = (
                    kept("y_codes_%d" % b, [P, 2, STORE_TILES * P], U32),
                    kept("y_plane_%d" % b, [P, 2, STORE_TILES * P], U8),
                )
            codes, plane = plane_tiles[b]
            cols = slice(place * P, (place + count) * P)
            nc.vector.quantize_mx(
                out=codes[:, g, cols].bitcast(FP8X4),
                scales=plane[:, g, cols],
                in_=y_grouped[b][:, g, 4 * cols.start : 4 * cols.stop],
            )

        def store_codes(first, count):
            b, place = divmod(first, STORE_TILES)
            nc.sync.dma_start(
                out=out_1[:, :, first * P : (first + count) * P, :].rearrange("g p n t -> p g (n t)").bitcast(I32),
                in_=plane_tiles[b][0][:, :, place * P : (place + count) * P].bitcast(I32),
            )

        def store_scales(b):
            cols = slice(b * STORE_TILES * P, (b + 1) * STORE_TILES * P)
            for quad in range(4):
                nc.sync.dma_start(
                    out=out_2[:, 4 * quad : 4 * quad + 4, cols].rearrange("g q n -> q g n").bitcast(I32),
                    in_=plane_tiles[b][1][32 * quad : 32 * quad + 4].bitcast(I32),
                )

        last = TILES - 1
        for step in range(TILES):
            units = units_of[step]
            light = step >= UNIT_STEPS
            on_gpsimd = step + 1 <= LAST_GPSIMD_GATE
            if on_gpsimd:
                gate_times_gain(nc.gpsimd, step + 1, 0)
            finish_y(step)
            if step % 2 == 0 and step + 6 < TILES:
                load_u(step + 6, 2)
            if step % 3 == 1 and step + 5 < TILES:
                pair = (step + 5) // 3
                load_gains(pair, rotating("v_raw", PASSES + pair, [P, 3, E], BF16, 4))
            if on_gpsimd:
                gate_times_gain(nc.gpsimd, step + 1, 1)
            elif step < last:
                for h in range(2):
                    gate_times_gain(nc.vector, step + 1, h)
            if units_of[step - 1] and not light:
                unit_square(units_of[step - 1][-1])
            if 1 <= step < last:
                for h in range(2):
                    for g in range(PASSES):
                        value_pass(step + 1, h, g)
            if step + 3 < TILES:
                sigmoid(step + 3)
            for place, (n, side) in enumerate(banks_of(step)):
                unit_relu(n, side)
                if place == 0 and len(units) == 2:
                    unit_scores(units[1], 1)
            if step == last:
                break
            nc.scalar.copy(*round_views(step, 1))
            if light:
                nc.scalar.copy(*round_views(step, 0))
            if len(units) == 2:
                unit_square(units[0])
            if step == UNIT_STEPS - 1:
                unit_square(units[-1])
            if step >= 1:
                turn_y(step - 1, range(2), "turn", 1)
            for n, side in banks_of(step + 1)[:3]:
                unit_scores(n, side)
            if not light:
                nc.vector.tensor_copy(*round_views(step, 0))
            if step in (5, 6, 9, 10):
                b, g = divmod(step - 5, STORE_TILES)
                quantize_y(b * STORE_TILES, STORE_TILES, g)
                if g == 1:
                    store_codes(b * STORE_TILES, STORE_TILES)
                    store_scales(b)
            if 1 <= step < UNIT_STEPS:
                quantize_units(step - 1)
            if step == UNIT_STEPS - 1:
                quantize_units(step)

        nc.scalar.copy(*round_views(last, 0))
        turn_y(last - 1, range(2), "turn", 1)
        nc.vector.tensor_copy(*round_views(last, 1))
        turn_y(last, range(0, 1), "scores", 3)
        turn_y(last, range(1, 2), "scores", 3)
        for g in range(2):
            quantize_y(last - 3, 2, g)
        for g in range(2):
            quantize_y(last - 1, 1, g)
        store_codes(last - 3, 3)
        for g in range(2):
            quantize_y(last, 1, g)
        store_codes(last, 1)
        store_scales(last // STORE_TILES)
